import numpy as np
import ml_dtypes

BF16 = ml_dtypes.bfloat16


def bf(x):
    return np.asarray(x, np.float32).astype(BF16)


def f32(x):
    return np.asarray(x, np.float32)


def f64(x):
    return np.asarray(x).astype(np.float64)


def striped(idx):
    return np.tile(idx.reshape(-1, 16).T, (8, 1))


S, K, M, N, H = 512, 128, 512, 192, 256


def sigmoid(v):
    return 1.0 / (1.0 + np.exp(-v))


def setup_inputs():
    return {"table": bf(np.random.standard_normal((S, K))), "w": bf(np.random.standard_normal((K, M)) / np.sqrt(K)), "offs": striped(np.random.permutation(np.tile(np.arange(S), 2))[:N])}


def reference(table, w, offs):
    idx = offs[:16].T.reshape(-1)
    x = f64(table)[idx].T
    y = f64(w).T @ x
    return y[:H] * sigmoid(y[H:])

@@ -1,0 +1,50 @@
+import concourse.mybir as mybir
+from concourse.masks import make_identity
+
+BF16, F32, U16 = mybir.dt.bfloat16, mybir.dt.float32, mybir.dt.uint16
+SIGMOID = mybir.ActivationFunctionType.Sigmoid
+
+P = 128
+S, K, M, N, H = 512, 128, 512, 192, 256
+
+FLOPS = 2 * K * M * N
+
+
+def tile_gather_matmul_kernel(tc, table, w, offs, out):
+    nc = tc.nc
+    with (
+        tc.tile_pool(name="held", bufs=1) as held,
+        tc.psum_pool(name="flip", bufs=1) as flip,
+        tc.psum_pool(name="prod", bufs=1) as prod,
+    ):
+        offsets = held.tile([P, N // 16], U16, name="offsets")
+        nc.sync.dma_start(offsets[:], offs)
+        words = held.tile([P, S // P, K], BF16, name="words")
+        nc.sync.dma_start(words[:], table.rearrange("(b p) k -> p b k", p=P))
+        weights = held.tile([K, M], BF16, name="weights")
+        nc.sync.dma_start(weights[:], w)
+
+        identity = held.tile([P, P], BF16, name="identity")
+        make_identity(nc, identity[:])
+        flipped = flip.tile([K, S], BF16, name="flipped")
+        for b in range(S // P):
+            nc.tensor.transpose(flipped[:, b * P : (b + 1) * P], words[:, b, :], identity[:])
+        features = held.tile([K, S], BF16, name="features")
+        nc.vector.tensor_copy(features[:], flipped[:])
+
+        y = [prod.tile([P, N], F32, name="y%d" % a) for a in range(M // P)]
+        for a in range(M // P):
+            nc.tensor.matmul(
+                y[a][:],
+                weights[:, a * P : (a + 1) * P],
+                features[:].indirect(offsets[:]),
+                start=True,
+                stop=True,
+            )
+
+        result = held.tile([P, H // P, N], F32, name="result")
+        for a in range(H // P):
+            gate = held.tile([P, N], F32, name="gate%d" % a)
+            nc.scalar.activation(gate[:], y[H // P + a][:], SIGMOID)
+            nc.vector.tensor_mul(result[:, a, :], y[a][:], gate[:])
+        nc.sync.dma_start(out.rearrange("(a p) j -> p a j", p=P), result[:])

@@ -17,34 +17,37 @@ def tile_gather_matmul_kernel(tc, table, w, offs, out):
         tc.psum_pool(name="flip", bufs=1) as flip,
         tc.psum_pool(name="prod", bufs=1) as prod,
     ):
+        blocks = table.rearrange("(h b p) k -> h p b k", h=2, p=P)
+        words = [held.tile([P, 2, K], BF16, name="words%d" % h) for h in range(2)]
+        nc.sync.dma_start(words[0][:], blocks[0])
+        nc.scalar.dma_start(words[1][:], blocks[1])
         offsets = held.tile([P, N // 16], U16, name="offsets")
         nc.sync.dma_start(offsets[:], offs)
-        words = held.tile([P, S // P, K], BF16, name="words")
-        nc.sync.dma_start(words[:], table.rearrange("(b p) k -> p b k", p=P))
         weights = held.tile([K, M], BF16, name="weights")
-        nc.sync.dma_start(weights[:], w)
+        nc.scalar.dma_start(weights[:], w)
 
         identity = held.tile([P, P], BF16, name="identity")
         make_identity(nc, identity[:])
-        flipped = flip.tile([K, S], BF16, name="flipped")
-        for b in range(S // P):
-            nc.tensor.transpose(flipped[:, b * P : (b + 1) * P], words[:, b, :], identity[:])
         features = held.tile([K, S], BF16, name="features")
-        nc.vector.tensor_copy(features[:], flipped[:])
+        for b in range(S // P):
+            flipped = flip.tile([K, P], BF16, name="flipped%d" % b)
+            nc.tensor.transpose(flipped[:], words[b // 2][:, b % 2, :], identity[:])
+            nc.vector.tensor_copy(features[:, b * P : (b + 1) * P], flipped[:])
 
-        y = [prod.tile([P, N], F32, name="y%d" % a) for a in range(M // P)]
-        for a in range(M // P):
-            nc.tensor.matmul(
-                y[a][:],
-                weights[:, a * P : (a + 1) * P],
-                features[:].indirect(offsets[:]),
-                start=True,
-                stop=True,
-            )
-
-        result = held.tile([P, H // P, N], F32, name="result")
+        rows = out.rearrange("(a p) j -> a p j", p=P)
         for a in range(H // P):
-            gate = held.tile([P, N], F32, name="gate%d" % a)
-            nc.scalar.activation(gate[:], y[H // P + a][:], SIGMOID)
-            nc.vector.tensor_mul(result[:, a, :], y[a][:], gate[:])
-        nc.sync.dma_start(out.rearrange("(a p) j -> p a j", p=P), result[:])
+            gates = prod.tile([P, N], F32, name="gates%d" % a)
+            values = prod.tile([P, N], F32, name="values%d" % a)
+            for y, c in ((gates, H // P + a), (values, a)):
+                nc.tensor.matmul(
+                    y[:],
+                    weights[:, c * P : (c + 1) * P],
+                    features[:].indirect(offsets[:]),
+                    start=True,
+                    stop=True,
+                )
+            opened = held.tile([P, N], F32, name="opened%d" % a)
+            nc.scalar.activation(opened[:], gates[:], SIGMOID)
+            result = held.tile([P, N], F32, name="result%d" % a)
+            nc.vector.tensor_mul(result[:], values[:], opened[:])
+            nc.sync.dma_start(rows[a], result[:])

@@ -9,14 +9,13 @@ S, K, M, N, H = 512, 128, 512, 192, 256
 
 FLOPS = 2 * K * M * N
 
+WARM_COLUMNS = 256
+WARM_MATMULS = 6
+
 
 def tile_gather_matmul_kernel(tc, table, w, offs, out):
     nc = tc.nc
-    with (
-        tc.tile_pool(name="held", bufs=1) as held,
-        tc.psum_pool(name="flip", bufs=1) as flip,
-        tc.psum_pool(name="prod", bufs=1) as prod,
-    ):
+    with tc.tile_pool(name="held", bufs=1) as held:
         blocks = table.rearrange("(h b p) k -> h p b k", h=2, p=P)
         words = [held.tile([P, 2, K], BF16, name="words%d" % h) for h in range(2)]
         nc.sync.dma_start(words[0][:], blocks[0])
@@ -26,28 +25,36 @@ def tile_gather_matmul_kernel(tc, table, w, offs, out):
         weights = held.tile([K, M], BF16, name="weights")
         nc.scalar.dma_start(weights[:], w)
 
-        identity = held.tile([P, P], BF16, name="identity")
-        make_identity(nc, identity[:])
-        features = held.tile([K, S], BF16, name="features")
-        for b in range(S // P):
-            flipped = flip.tile([K, P], BF16, name="flipped%d" % b)
-            nc.tensor.transpose(flipped[:], words[b // 2][:, b % 2, :], identity[:])
-            nc.vector.tensor_copy(features[:, b * P : (b + 1) * P], flipped[:])
+        with tc.psum_pool(name="early", bufs=1) as early:
+            zeros = held.tile([P, WARM_COLUMNS], BF16, name="zeros")
+            nc.vector.memset(zeros[:], 0.0)
+            unread = early.tile([P, WARM_COLUMNS], F32, name="unread")
+            for i in range(WARM_MATMULS):
+                nc.tensor.matmul(unread[:], zeros[:, 0:P], zeros[:], start=True, stop=True)
+
+            identity = held.tile([P, P], BF16, name="identity")
+            make_identity(nc, identity[:])
+            features = held.tile([K, S], BF16, name="features")
+            for b in range(S // P):
+                flipped = early.tile([K, P], BF16, name="flipped%d" % b)
+                nc.tensor.transpose(flipped[:], words[b // 2][:, b % 2, :], identity[:])
+                nc.vector.tensor_copy(features[:, b * P : (b + 1) * P], flipped[:])
 
         rows = out.rearrange("(a p) j -> a p j", p=P)
-        for a in range(H // P):
-            gates = prod.tile([P, N], F32, name="gates%d" % a)
-            values = prod.tile([P, N], F32, name="values%d" % a)
-            for y, c in ((gates, H // P + a), (values, a)):
-                nc.tensor.matmul(
-                    y[:],
-                    weights[:, c * P : (c + 1) * P],
-                    features[:].indirect(offsets[:]),
-                    start=True,
-                    stop=True,
-                )
-            opened = held.tile([P, N], F32, name="opened%d" % a)
-            nc.scalar.activation(opened[:], gates[:], SIGMOID)
-            result = held.tile([P, N], F32, name="result%d" % a)
-            nc.vector.tensor_mul(result[:], values[:], opened[:])
-            nc.sync.dma_start(rows[a], result[:])
+        with tc.psum_pool(name="prod", bufs=1) as prod:
+            for a in range(H // P):
+                gates = prod.tile([P, N], F32, name="gates%d" % a)
+                values = prod.tile([P, N], F32, name="values%d" % a)
+                for y, c in ((gates, H // P + a), (values, a)):
+                    nc.tensor.matmul(
+                        y[:],
+                        weights[:, c * P : (c + 1) * P],
+                        features[:].indirect(offsets[:]),
+                        start=True,
+                        stop=True,
+                    )
+                opened = held.tile([P, N], F32, name="opened%d" % a)
+                nc.scalar.activation(opened[:], gates[:], SIGMOID)
+                result = held.tile([P, N], F32, name="result%d" % a)
+                nc.vector.tensor_mul(result[:], values[:], opened[:])
+                nc.sync.dma_start(rows[a], result[:])

@@ -9,52 +9,43 @@ S, K, M, N, H = 512, 128, 512, 192, 256
 
 FLOPS = 2 * K * M * N
 
-WARM_COLUMNS = 256
-WARM_MATMULS = 6
+BLOCKS = S // P
 
 
 def tile_gather_matmul_kernel(tc, table, w, offs, out):
     nc = tc.nc
-    with tc.tile_pool(name="held", bufs=1) as held:
-        blocks = table.rearrange("(h b p) k -> h p b k", h=2, p=P)
-        words = [held.tile([P, 2, K], BF16, name="words%d" % h) for h in range(2)]
-        nc.sync.dma_start(words[0][:], blocks[0])
-        nc.scalar.dma_start(words[1][:], blocks[1])
+    with tc.tile_pool(name="held", bufs=1) as held, tc.psum_pool(name="banks", bufs=1) as banks:
+        halves = table.rearrange("(h b p) k -> h p b k", h=2, p=P)
+        words = [held.tile([P, BLOCKS // 2, K], BF16, name="words%d" % h) for h in range(2)]
+        nc.sync.dma_start(words[0][:], halves[0])
+        nc.scalar.dma_start(words[1][:], halves[1])
         offsets = held.tile([P, N // 16], U16, name="offsets")
         nc.sync.dma_start(offsets[:], offs)
         weights = held.tile([K, M], BF16, name="weights")
         nc.scalar.dma_start(weights[:], w)
 
-        with tc.psum_pool(name="early", bufs=1) as early:
-            zeros = held.tile([P, WARM_COLUMNS], BF16, name="zeros")
-            nc.vector.memset(zeros[:], 0.0)
-            unread = early.tile([P, WARM_COLUMNS], F32, name="unread")
-            for i in range(WARM_MATMULS):
-                nc.tensor.matmul(unread[:], zeros[:, 0:P], zeros[:], start=True, stop=True)
-
-            identity = held.tile([P, P], BF16, name="identity")
-            make_identity(nc, identity[:])
-            features = held.tile([K, S], BF16, name="features")
-            for b in range(S // P):
-                flipped = early.tile([K, P], BF16, name="flipped%d" % b)
-                nc.tensor.transpose(flipped[:], words[b // 2][:, b % 2, :], identity[:])
-                nc.vector.tensor_copy(features[:, b * P : (b + 1) * P], flipped[:])
+        identity = held.tile([P, P], BF16, name="identity")
+        make_identity(nc, identity[:])
+        features = held.tile([K, S], BF16, name="features")
+        for b in range(BLOCKS):
+            flipped = banks.tile([K, P], BF16, name="flipped%d" % b)
+            nc.tensor.transpose(flipped[:], words[b // 2][:, b % 2, :], identity[:])
+            nc.vector.tensor_copy(features[:, b * P : (b + 1) * P], flipped[:])
 
         rows = out.rearrange("(a p) j -> a p j", p=P)
-        with tc.psum_pool(name="prod", bufs=1) as prod:
-            for a in range(H // P):
-                gates = prod.tile([P, N], F32, name="gates%d" % a)
-                values = prod.tile([P, N], F32, name="values%d" % a)
-                for y, c in ((gates, H // P + a), (values, a)):
-                    nc.tensor.matmul(
-                        y[:],
-                        weights[:, c * P : (c + 1) * P],
-                        features[:].indirect(offsets[:]),
-                        start=True,
-                        stop=True,
-                    )
-                opened = held.tile([P, N], F32, name="opened%d" % a)
-                nc.scalar.activation(opened[:], gates[:], SIGMOID)
-                result = held.tile([P, N], F32, name="result%d" % a)
-                nc.vector.tensor_mul(result[:], values[:], opened[:])
-                nc.sync.dma_start(rows[a], result[:])
+        for a in range(H // P):
+            gates = banks.tile([P, N], F32, name="gates%d" % a)
+            values = banks.tile([P, N], F32, name="values%d" % a)
+            for y, c in ((gates, H // P + a), (values, a)):
+                nc.tensor.matmul(
+                    y[:],
+                    weights[:, c * P : (c + 1) * P],
+                    features[:].indirect(offsets[:]),
+                    start=True,
+                    stop=True,
+                )
+            opened = held.tile([P, N], F32, name="opened%d" % a)
+            nc.scalar.activation(opened[:], gates[:], SIGMOID)
+            result = held.tile([P, N], F32, name="result%d" % a)
+            nc.vector.tensor_mul(result[:], values[:], opened[:])
+            nc.sync.dma_start(rows[a], result[:])

import concourse.mybir as mybir
from concourse.masks import make_identity

BF16, F32, U16 = mybir.dt.bfloat16, mybir.dt.float32, mybir.dt.uint16
SIGMOID = mybir.ActivationFunctionType.Sigmoid

P = 128
S, K, M, N, H = 512, 128, 512, 192, 256

FLOPS = 2 * K * M * N

BLOCKS = S // P


def tile_gather_matmul_kernel(tc, table, w, offs, out):
    nc = tc.nc
    with tc.tile_pool(name="held", bufs=1) as held, tc.psum_pool(name="banks", bufs=1) as banks:
        halves = table.rearrange("(h b p) k -> h p b k", h=2, p=P)
        words = [held.tile([P, BLOCKS // 2, K], BF16, name="words%d" % h) for h in range(2)]
        nc.sync.dma_start(words[0][:], halves[0])
        nc.scalar.dma_start(words[1][:], halves[1])
        offsets = held.tile([P, N // 16], U16, name="offsets")
        nc.sync.dma_start(offsets[:], offs)
        weights = held.tile([K, M], BF16, name="weights")
        nc.scalar.dma_start(weights[:], w)

        identity = held.tile([P, P], BF16, name="identity")
        make_identity(nc, identity[:])
        features = held.tile([K, S], BF16, name="features")
        for b in range(BLOCKS):
            flipped = banks.tile([K, P], BF16, name="flipped%d" % b)
            nc.tensor.transpose(flipped[:], words[b // 2][:, b % 2, :], identity[:])
            nc.vector.tensor_copy(features[:, b * P : (b + 1) * P], flipped[:])

        rows = out.rearrange("(a p) j -> a p j", p=P)
        for a in range(H // P):
            gates = banks.tile([P, N], F32, name="gates%d" % a)
            values = banks.tile([P, N], F32, name="values%d" % a)
            for y, c in ((gates, H // P + a), (values, a)):
                nc.tensor.matmul(
                    y[:],
                    weights[:, c * P : (c + 1) * P],
                    features[:].indirect(offsets[:]),
                    start=True,
                    stop=True,
                )
            opened = held.tile([P, N], F32, name="opened%d" % a)
            nc.scalar.activation(opened[:], gates[:], SIGMOID)
            result = held.tile([P, N], F32, name="result%d" % a)
            nc.vector.tensor_mul(result[:], values[:], opened[:])
            nc.sync.dma_start(rows[a], result[:])
